import numpy as np
import ml_dtypes


def mxq(x, axis, fmt="e4m3"):
    dtype, down = {"e4m3": (ml_dtypes.float8_e4m3fn, 7), "e5m2": (ml_dtypes.float8_e5m2, 14)}[fmt]
    v = np.moveaxis(np.asarray(x, np.float32).astype(ml_dtypes.bfloat16).astype(np.float64), axis, -1)
    blocks = v.reshape(v.shape[:-1] + (-1, 32))
    amax = np.abs(blocks).max(-1, keepdims=True)
    byte = np.maximum(np.where(amax > 0, np.frexp(amax)[1] - 1 + 127, 0) - down, 1)
    scale = np.exp2(byte - 127.0)
    codes = (blocks / scale).astype(np.float32).astype(dtype).astype(np.float64)
    return np.moveaxis((codes * scale).reshape(v.shape), -1, axis)


WIDE = False


def mx_kscale(k):
    if not WIDE:
        return np.ones(k)
    levels = np.array([10, -10, 5, -5, 0])
    if k % 512:
        return np.exp2(np.random.permutation(np.resize(levels, k // 32))).repeat(32)
    a = np.empty((k // 512, 16))
    for p in range(k // 512):
        a[p, :8] = np.random.permutation(np.resize(levels, 8))
        for g in range(8):
            far = levels[np.abs(levels - a[p, g]) >= 10]
            a[p, g + 8] = far[np.random.randint(len(far))]
    return np.exp2(a.ravel()).repeat(32)


def f64(x):
    return np.asarray(x).astype(np.float64)


def striped(idx):
    return np.tile(idx.reshape(-1, 16).T, (8, 1)).astype(np.uint16)


def unstriped(offs):
    return offs[:16].T.reshape(-1).astype(np.int64)


def striped8(idx):
    return np.concatenate([x.reshape(-1, 16).T for x in idx]).astype(np.uint16)


def runs(offs, k):
    lists = np.stack([offs[16 * r : 16 * r + 16].T.reshape(-1) for r in range(8)]).astype(np.int64)
    return lists[np.arange(k) % 512 // 64]


def pack_weight(w):
    k, n = w.shape
    w = f64(np.asarray(w, np.float32).astype(ml_dtypes.bfloat16)).reshape(k // 32, 32, n)
    amax = np.abs(w).max(1)
    byte = np.clip(np.where(amax > 0, np.frexp(amax)[1] - 1 + 127 - 7, 1), 1, 254)
    scaled = (w * np.exp2(127.0 - byte)[:, None, :]).reshape(k, n).astype(np.float32)
    words = np.ascontiguousarray(scaled.reshape(k // 512, 128, 4, n).transpose(0, 1, 3, 2)).astype(ml_dtypes.float8_e4m3fn).view(np.uint8)
    return words, np.ascontiguousarray(byte.astype(np.uint8).reshape(k // 512, 16, n))


def unpack_weight(words, scales):
    g, p, n, _ = words.shape
    vals = np.ascontiguousarray(words).view(ml_dtypes.float8_e4m3fn).astype(np.float64) * np.repeat(np.exp2(scales.astype(np.float64) - 127.0), 8, axis=1)[..., None]
    return vals.transpose(0, 1, 3, 2).reshape(g * 512, n)

def planes(y):
    n, m = y.shape
    v = y.astype(np.float32).astype(ml_dtypes.bfloat16).astype(np.float64).reshape(n // 32, 32, m)
    top = np.abs(v).max(1)
    byte = np.clip(np.where(top > 0, np.frexp(top)[1] - 1 + 127 - 7, 1), 1, 254)
    codes = (v * np.exp2(127.0 - byte)[:, None, :]).reshape(n, m).astype(np.float32).astype(ml_dtypes.float8_e4m3fn).view(np.uint8)
    words = codes.reshape(n // 512, 128, 4, m).transpose(0, 1, 3, 2)
    return np.ascontiguousarray(words), np.ascontiguousarray(byte.astype(np.uint8).reshape(n // 512, 16, m))


K, T, S, N, G, H, U = 512, 2048, 512, 512, 2048, 512, 1024


def setup_inputs():
    n = np.random.standard_normal
    s = mx_kscale(K)[:, None]
    u = mx_kscale(H)
    packed_xT = pack_weight(n((K, T)) * s)
    packed_dT = pack_weight(n((K, G)) / s)
    packed_w1 = pack_weight(n((H, N)) / np.sqrt(H) / u[:, None])
    return {
        "x_words": packed_xT[0],
        "x_scales": packed_xT[1],
        "d_words": packed_dT[0],
        "d_scales": packed_dT[1],
        "old": n((H, U)).astype(np.float32),
        "gn": (np.random.uniform(0.5, 1.5, (H, 1)) * u[:, None]).astype(np.float32),
        "w1_words": packed_w1[0],
        "w1_scales": packed_w1[1],
        "offs": striped(np.random.permutation(T)[:S]),
        "kidx": striped8(np.random.randint(0, G, (8, H))),
        "slot": striped8(np.stack([np.random.permutation(U)[:S] for _ in range(8)])),
    }


def reference(x_words, x_scales, d_words, d_scales, old, gn, w1_words, w1_scales, offs, kidx, slot):
    d_kidx = unpack_weight(d_words, d_scales)[np.arange(K)[:, None], runs(kidx, K)]
    xq = unpack_weight(x_words, x_scales)[:, unstriped(offs)]
    s = 0.0625 * (d_kidx.T @ xq)
    nw = np.maximum(s, 0.5 * (f64(old)[np.arange(H)[:, None], runs(slot, H)]))
    pg = f64(old).copy()
    pg[np.arange(H)[:, None], runs(slot, H)] = nw
    z = f64(gn) * pg
    out_0 = unpack_weight(w1_words, w1_scales).T @ mxq(z, 0, "e4m3")
    return (out_0,) + planes(out_0)

@@ -1,0 +1,224 @@
+from contextlib import ExitStack
+
+import concourse.mybir as mybir
+
+F32 = mybir.dt.float32
+BF16 = mybir.dt.bfloat16
+I32 = mybir.dt.int32
+U32 = mybir.dt.uint32
+U16 = mybir.dt.uint16
+U8 = mybir.dt.uint8
+FP8X4 = mybir.dt.float8_e4m3fn_x4
+ALU = mybir.AluOpType
+COPY = mybir.ActivationFunctionType.Copy
+
+P = 128
+PACK = 4
+TABLE = 2048
+PICKED = 512
+SLOTS = 1024
+STRIP = 128
+HALF = SLOTS // 2
+WEIGH = ((0, 128), (128, 128), (512, 256), (256, 256), (768, 256))
+CHUNKS = ((0, 128), (128, 128), (512, 256), (256, 256), (768, 128), (896, 128))
+
+FLOPS = 2 * 512 * 512 * 512 + 2 * 512 * 512 * 1024
+
+
+def words_of(dram_words):
+    return dram_words[0].rearrange("p n r -> p (n r)").bitcast(I32)
+
+
+def deal(nc, out, in_):
+    nc.vector.tensor_copy(out=out.rearrange("p (t m) -> p m t", t=PACK), in_=in_.rearrange("p (m t) -> p m t", t=PACK))
+
+
+def tile_picked_scorepage_none_po_kernel(
+    tc, x_words, x_scales, d_words, d_scales, old, gn, w1_words, w1_scales, offs, kidx, slot, out_0, out_1, out_2
+):
+    nc = tc.nc
+    with ExitStack() as ctx:
+        keep = ctx.enter_context(tc.tile_pool(name="keep", bufs=1))
+        psum = ctx.enter_context(tc.psum_pool(name="psum", bufs=8))
+
+        def sbuf(name, shape, dtype, tag=None):
+            return keep.tile(shape, dtype, name=name, tag=tag or name, align_bytes=64)
+
+        kidx_sb = keep.tile([P, PICKED // 16], U16, name="kidx_sb")
+        slot_sb = keep.tile([P, PICKED // 16], U16, name="slot_sb")
+        offs_sb = keep.tile([P, PICKED // 16], U16, name="offs_sb")
+        d_tab = sbuf("d_tab", [P, TABLE], U32)
+        x_tab = sbuf("x_tab", [P, TABLE], U32)
+        d_stab = sbuf("d_stab", [P, TABLE], U8, "A")
+        x_stab = sbuf("x_stab", [P, TABLE], U8, "C")
+        gn_sb = sbuf("gn_sb", [P, PACK], F32)
+        gn_early = sbuf("gn_early", [P, PACK], F32, "G")
+        page = [sbuf(f"page{t}", [P, SLOTS], F32) for t in range(3)]
+        old_rows = old.rearrange("(p t) w -> t p w", t=PACK)
+
+        nc.vector.memset(d_stab[:].bitcast(I32), 0)
+        nc.gpsimd.memset(x_stab[:].bitcast(I32), 0)
+
+        nc.sync.dma_start(slot_sb[:], slot)
+        nc.sync.dma_start(page[0][:], old_rows[0])
+        nc.sync.dma_start(kidx_sb[:], kidx)
+        d_rows = d_scales[0].bitcast(I32).rearrange("(r a) n -> a r n", a=2)
+        for a in range(2):
+            nc.sync.dma_start(d_stab[a:P:16, :].bitcast(I32), d_rows[a])
+        nc.sync.dma_start(d_tab[:].bitcast(I32), words_of(d_words))
+        nc.sync.dma_start(offs_sb[:], offs)
+        x_rows = x_scales[0].bitcast(I32).rearrange("(q a) n -> a q n", a=4)
+        for a in range(4):
+            nc.sync.dma_start(x_stab[a:P:32, :].bitcast(I32), x_rows[a])
+        nc.sync.dma_start(x_tab[:].bitcast(I32), words_of(x_words))
+        nc.sync.dma_start(page[1][:], old_rows[1])
+        nc.sync.dma_start(page[2][:], old_rows[2])
+        for gains in (gn_sb, gn_early):
+            nc.gpsimd.dma_start(gains[:], gn.rearrange("(p t) o -> p (t o)", t=PACK))
+
+        half = {}
+
+        def fetch(t, tag=None):
+            half[t] = sbuf(f"half{t}", [P, PICKED], F32, tag)
+            nc.vector.tensor_scalar(half[t][:], page[t][:].indirect(slot_sb[:]), 0.5, 0.0, ALU.mult, ALU.add)
+
+        fetch(0)
+        d_sgot = sbuf("d_sgot", [P, PICKED], U8, "B")
+        d_sc = sbuf("d_sc", [P, PICKED], U8)
+        nc.vector.tensor_copy(d_sgot[:], d_stab[:].indirect(kidx_sb[:]))
+        deal(nc, d_sc[:], d_sgot[:])
+        for a in range(2):
+            nc.scalar.dma_start(d_sc[2 + a : P : 32, :].bitcast(I32), d_sc[16 + a : P : 32, :].bitcast(I32))
+        page.append(sbuf("page3", [P, SLOTS], F32, "B"))
+        nc.sync.dma_start(page[3][:], old_rows[3])
+
+        d_got = sbuf("d_got", [P, PICKED], U32, "D")
+        d_codes = sbuf("d_codes", [P, PICKED], U32)
+        nc.vector.tensor_copy(d_got[:], d_tab[:].indirect(kidx_sb[:]))
+        x_sc = sbuf("x_sc", [P, PICKED], U8)
+        nc.vector.tensor_copy(x_sc[:], x_stab[:].indirect(offs_sb[:]))
+        w_raw = sbuf("w_raw", [P, PICKED], U32, "C")
+        nc.sync.dma_start(w_raw[:].bitcast(I32), words_of(w1_words))
+        deal(nc, d_codes[:].bitcast(I32), d_got[:].bitcast(I32))
+        w_sraw = sbuf("w_sraw", [P, PICKED], U8, "D")
+        nc.gpsimd.memset(w_sraw[:].bitcast(I32), 0)
+        w_rows = w1_scales[0].bitcast(I32).rearrange("(q a) n -> a q n", a=4)
+        for a in range(4):
+            nc.sync.dma_start(w_sraw[a:P:32, :].bitcast(I32), w_rows[a])
+        x_codes = sbuf("x_codes", [P, PICKED], U32)
+        nc.vector.tensor_copy(x_codes[:], x_tab[:].indirect(offs_sb[:]))
+
+        scores = []
+        for t in range(PACK):
+            bank = psum.tile([P, PICKED], F32, name="bank")
+            cols = slice(t * P, (t + 1) * P)
+            nc.tensor.matmul_mx(
+                out=bank[:], lhsT=d_codes[:, cols].bitcast(FP8X4), lhsT_scale=d_sc[:, cols],
+                rhs=x_codes[:].bitcast(FP8X4), rhs_scale=x_sc[:], start=True, stop=True,
+            )
+            scores.append(bank)
+
+        z_bf = [sbuf(f"z_bf{h}", [P, HALF * PACK], BF16) for h in range(2)]
+
+        def z_plane(t, start, width):
+            at = start % HALF
+            return z_bf[start // HALF][:].rearrange("p (w t) -> p w t", t=PACK)[:, at : at + width, t]
+
+        new = {}
+
+        def larger(t, tag=None):
+            new[t] = sbuf(f"new{t}", [P, PICKED], F32, tag)
+            nc.vector.scalar_tensor_tensor(new[t][:], scores[t][:], 0.0625, half[t][:], ALU.mult, ALU.max)
+
+        def put(t):
+            nc.vector.tensor_copy(page[t][:].indirect(slot_sb[:]), new[t][:])
+
+        def weigh_on_scalar(t, start, width, gains):
+            nc.scalar.activation(z_plane(t, start, width), page[t][:, start : start + width], COPY, scale=gains[:, t : t + 1])
+
+        def weigh_early(t):
+            weigh_on_scalar(t, 0, HALF, gn_early)
+            weigh_on_scalar(t, HALF, HALF, gn_sb)
+
+        def weigh_last(start, width):
+            t = PACK - 1
+            if start >= HALF:
+                weigh_on_scalar(t, start, width, gn_sb)
+            else:
+                nc.vector.tensor_scalar(
+                    z_plane(t, start, width), page[t][:, start : start + width], gn_sb[:, t : t + 1], None, ALU.mult
+                )
+
+        fetch(1)
+        fetch(2)
+        larger(0, "N0")
+        larger(1, "N1")
+        put(0)
+        weigh_early(0)
+        larger(2, "N2")
+        put(1)
+        weigh_early(1)
+        put(2)
+        weigh_early(2)
+        fetch(3, "N2")
+        w_codes = sbuf("w_codes", [P, PICKED], U32, "N1")
+        w_sc = sbuf("w_sc", [P, PICKED], U8, "N0")
+        deal(nc, w_codes[:].bitcast(I32), w_raw[:].bitcast(I32))
+        larger(3, "G")
+        deal(nc, w_sc[:], w_sraw[:])
+        put(3)
+
+        y_sc = sbuf("y_sc", [P, SLOTS], U8)
+        out_rows = out_0.rearrange("(p t) w -> p t w", t=PACK)
+        out_words = words_of(out_1)
+        banks = {}
+
+        def product(start, width):
+            z_codes = sbuf(f"z_codes{start}", [P, width], U32)
+            z_sc = sbuf(f"z_sc{start}", [P, width], U8)
+            at = start % HALF * PACK
+            nc.vector.quantize_mx(
+                out=z_codes[:].bitcast(FP8X4), scales=z_sc[:], in_=z_bf[start // HALF][:, at : at + width * PACK]
+            )
+            for s in range(0, width, STRIP):
+                bank = psum.tile([P, PACK, STRIP], F32, name="bank")
+                banks[start + s] = bank
+                strip = slice(s, s + STRIP)
+                for t in range(PACK):
+                    cols = slice(t * P, (t + 1) * P)
+                    nc.tensor.matmul_mx(
+                        out=bank[:, t, :], lhsT=w_codes[:, cols].bitcast(FP8X4), lhsT_scale=w_sc[:, cols],
+                        rhs=z_codes[:, strip].bitcast(FP8X4), rhs_scale=z_sc[:, strip], start=True, stop=True,
+                    )
+
+        y = {}
+        y_bf = {}
+
+        def leave(start, width):
+            y[start] = sbuf(f"y{start}", [P, PACK, width], F32)
+            for s in range(0, width, STRIP):
+                nc.scalar.copy(y[start][:, :, s : s + STRIP], banks[start + s][:])
+            nc.sync.dma_start(out_rows[:, :, start : start + width], y[start][:])
+
+        def weave(start, width):
+            y_bf[start] = sbuf(f"y_bf{start}", [P, width * PACK], BF16)
+            nc.vector.tensor_copy(
+                out=y_bf[start][:].rearrange("p (g i t) -> p g t i", i=4, t=PACK),
+                in_=y[start][:].rearrange("p t (g i) -> p g t i", i=4),
+            )
+
+        def planes(start, width):
+            cols = slice(start, start + width)
+            y_codes = sbuf(f"y_codes{start}", [P, width], U32)
+            nc.vector.quantize_mx(out=y_codes[:].bitcast(FP8X4), scales=y_sc[:, cols], in_=y_bf[start][:])
+            nc.sync.dma_start(out_words[:, cols], y_codes[:].bitcast(I32))
+
+        stages = ((weigh_last, WEIGH), (product, WEIGH), (leave, CHUNKS), (weave, CHUNKS), (planes, CHUNKS))
+        for step in range(len(CHUNKS) + len(stages) - 1):
+            for lag, (stage, spans) in enumerate(stages):
+                if 0 <= step - lag < len(spans):
+                    stage(*spans[step - lag])
+        out_srows = out_2[0].bitcast(I32).rearrange("(q a) n -> a q n", a=4)
+        for a in range(4):
+            queue = nc.scalar if a % 2 else nc.sync
+            queue.dma_start(out_srows[a], y_sc[a:P:32, :].bitcast(I32))

@@ -19,8 +19,8 @@ PICKED = 512
 SLOTS = 1024
 STRIP = 128
 HALF = SLOTS // 2
-WEIGH = ((0, 128), (128, 128), (512, 256), (256, 256), (768, 256))
-CHUNKS = ((0, 128), (128, 128), (512, 256), (256, 256), (768, 128), (896, 128))
+CHUNKS = ((0, 128), (128, 128), (512, 256), (256, 256), (768, 256))
+BANK = 512
 
 FLOPS = 2 * 512 * 512 * 512 + 2 * 512 * 512 * 1024
 
@@ -51,8 +51,8 @@ def tile_picked_scorepage_none_po_kernel(
         x_tab = sbuf("x_tab", [P, TABLE], U32)
         d_stab = sbuf("d_stab", [P, TABLE], U8, "A")
         x_stab = sbuf("x_stab", [P, TABLE], U8, "C")
-        gn_sb = sbuf("gn_sb", [P, PACK], F32)
-        gn_early = sbuf("gn_early", [P, PACK], F32, "G")
+        gn_sb = sbuf("gn_sb", [P, PACK], F32, "G")
+        gn_kept = sbuf("gn_kept", [P, 1], F32)
         page = [sbuf(f"page{t}", [P, SLOTS], F32) for t in range(3)]
         old_rows = old.rearrange("(p t) w -> t p w", t=PACK)
 
@@ -73,8 +73,8 @@ def tile_picked_scorepage_none_po_kernel(
         nc.sync.dma_start(x_tab[:].bitcast(I32), words_of(x_words))
         nc.sync.dma_start(page[1][:], old_rows[1])
         nc.sync.dma_start(page[2][:], old_rows[2])
-        for gains in (gn_sb, gn_early):
-            nc.gpsimd.dma_start(gains[:], gn.rearrange("(p t) o -> p (t o)", t=PACK))
+        nc.gpsimd.dma_start(gn_sb[:], gn.rearrange("(p t) o -> p (t o)", t=PACK))
+        nc.scalar.copy(gn_kept[:], gn_sb[:, PACK - 1 : PACK])
 
         half = {}
 
@@ -134,39 +134,41 @@ def tile_picked_scorepage_none_po_kernel(
             nc.vector.tensor_copy(page[t][:].indirect(slot_sb[:]), new[t][:])
 
         def weigh_on_scalar(t, start, width, gains):
-            nc.scalar.activation(z_plane(t, start, width), page[t][:, start : start + width], COPY, scale=gains[:, t : t + 1])
+            nc.scalar.activation(z_plane(t, start, width), page[t][:, start : start + width], COPY, scale=gains)
 
         def weigh_early(t):
-            weigh_on_scalar(t, 0, HALF, gn_early)
-            weigh_on_scalar(t, HALF, HALF, gn_sb)
+            weigh_on_scalar(t, 0, HALF, gn_sb[:, t : t + 1])
+            weigh_on_scalar(t, HALF, HALF, gn_sb[:, t : t + 1])
 
         def weigh_last(start, width):
             t = PACK - 1
             if start >= HALF:
-                weigh_on_scalar(t, start, width, gn_sb)
+                weigh_on_scalar(t, start, width, gn_last[:])
             else:
                 nc.vector.tensor_scalar(
-                    z_plane(t, start, width), page[t][:, start : start + width], gn_sb[:, t : t + 1], None, ALU.mult
+                    z_plane(t, start, width), page[t][:, start : start + width], gn_last[:], None, ALU.mult
                 )
 
         fetch(1)
-        fetch(2)
         larger(0, "N0")
         larger(1, "N1")
         put(0)
         weigh_early(0)
-        larger(2, "N2")
+        fetch(2, "N0")
         put(1)
         weigh_early(1)
+        larger(2, "N2")
+        fetch(3, "N1")
         put(2)
         weigh_early(2)
-        fetch(3, "N2")
-        w_codes = sbuf("w_codes", [P, PICKED], U32, "N1")
-        w_sc = sbuf("w_sc", [P, PICKED], U8, "N0")
+        gn_last = sbuf("gn_last", [P, 1], F32, "G")
+        nc.scalar.copy(gn_last[:], gn_kept[:])
+        larger(3, "N3")
+        w_codes = sbuf("w_codes", [P, PICKED], U32, "N2")
         deal(nc, w_codes[:].bitcast(I32), w_raw[:].bitcast(I32))
-        larger(3, "G")
-        deal(nc, w_sc[:], w_sraw[:])
         put(3)
+        w_sc = sbuf("w_sc", [P, PICKED], U8, "N3")
+        deal(nc, w_sc[:], w_sraw[:])
 
         y_sc = sbuf("y_sc", [P, SLOTS], U8)
         out_rows = out_0.rearrange("(p t) w -> p t w", t=PACK)
@@ -180,44 +182,63 @@ def tile_picked_scorepage_none_po_kernel(
             nc.vector.quantize_mx(
                 out=z_codes[:].bitcast(FP8X4), scales=z_sc[:], in_=z_bf[start // HALF][:, at : at + width * PACK]
             )
-            for s in range(0, width, STRIP):
-                bank = psum.tile([P, PACK, STRIP], F32, name="bank")
-                banks[start + s] = bank
-                strip = slice(s, s + STRIP)
+            n = STRIP if start == CHUNKS[-1][0] else width
+            banks[start] = []
+            for s in range(0, width, n):
+                strip = slice(s, s + n)
                 for t in range(PACK):
+                    if t % (BANK // n) == 0:
+                        bank = psum.tile([P, BANK // n, n], F32, name="bank")
+                        banks[start].append((bank, slice(t, t + BANK // n), strip))
                     cols = slice(t * P, (t + 1) * P)
                     nc.tensor.matmul_mx(
-                        out=bank[:, t, :], lhsT=w_codes[:, cols].bitcast(FP8X4), lhsT_scale=w_sc[:, cols],
+                        out=bank[:, t % (BANK // n), :], lhsT=w_codes[:, cols].bitcast(FP8X4), lhsT_scale=w_sc[:, cols],
                         rhs=z_codes[:, strip].bitcast(FP8X4), rhs_scale=z_sc[:, strip], start=True, stop=True,
                     )
 
         y = {}
         y_bf = {}
+        y_codes = sbuf("y_codes", [P, SLOTS], U32)
+        last = CHUNKS[-1][0]
 
-        def leave(start, width):
-            y[start] = sbuf(f"y{start}", [P, PACK, width], F32)
-            for s in range(0, width, STRIP):
-                nc.scalar.copy(y[start][:, :, s : s + STRIP], banks[start + s][:])
-            nc.sync.dma_start(out_rows[:, :, start : start + width], y[start][:])
-
-        def weave(start, width):
+        def weave_from(start, source):
+            width = source.shape[-1]
             y_bf[start] = sbuf(f"y_bf{start}", [P, width * PACK], BF16)
             nc.vector.tensor_copy(
                 out=y_bf[start][:].rearrange("p (g i t) -> p g t i", i=4, t=PACK),
-                in_=y[start][:].rearrange("p t (g i) -> p g t i", i=4),
+                in_=source.rearrange("p t (g i) -> p g t i", i=4),
             )
 
-        def planes(start, width):
-            cols = slice(start, start + width)
-            y_codes = sbuf(f"y_codes{start}", [P, width], U32)
-            nc.vector.quantize_mx(out=y_codes[:].bitcast(FP8X4), scales=y_sc[:, cols], in_=y_bf[start][:])
-            nc.sync.dma_start(out_words[:, cols], y_codes[:].bitcast(I32))
+        def leave(start, width):
+            y[start] = sbuf(f"y{start}", [P, PACK, width], F32)
+            for bank, rows, strip in banks[start]:
+                if start + strip.stop == SLOTS:
+                    y_bf[SLOTS - STRIP] = sbuf("y_bf_last", [P, STRIP * PACK], BF16)
+                    nc.scalar.copy(
+                        out=y_bf[SLOTS - STRIP][:].rearrange("p (w t) -> p w t", t=PACK),
+                        in_=bank[:].rearrange("p t w -> p w t"),
+                    )
+                nc.scalar.copy(y[start][:, rows, strip], bank[:])
+            nc.sync.dma_start(out_rows[:, :, start : start + width], y[start][:])
 
-        stages = ((weigh_last, WEIGH), (product, WEIGH), (leave, CHUNKS), (weave, CHUNKS), (planes, CHUNKS))
+        def weave(start, width):
+            weave_from(start, y[start][:, :, 0:STRIP] if start == last else y[start][:])
+
+        def planes(start, width):
+            parts = (start, start + STRIP) if start == last else (start,)
+            for at in parts:
+                cols = slice(at, at + width // len(parts))
+                nc.vector.quantize_mx(out=y_codes[:, cols].bitcast(FP8X4), scales=y_sc[:, cols], in_=y_bf[at][:])
+            if start == CHUNKS[-2][0]:
+                nc.sync.dma_start(out_words[:, 0:last], y_codes[:, 0:last].bitcast(I32))
+            if start == last:
+                nc.sync.dma_start(out_words[:, last:SLOTS], y_codes[:, last:SLOTS].bitcast(I32))
+
+        stages = (weigh_last, product, leave, weave, planes)
         for step in range(len(CHUNKS) + len(stages) - 1):
-            for lag, (stage, spans) in enumerate(stages):
-                if 0 <= step - lag < len(spans):
-                    stage(*spans[step - lag])
+            for lag, stage in enumerate(stages):
+                if 0 <= step - lag < len(CHUNKS):
+                    stage(*CHUNKS[step - lag])
         out_srows = out_2[0].bitcast(I32).rearrange("(q a) n -> a q n", a=4)
         for a in range(4):
             queue = nc.scalar if a % 2 else nc.sync

@@ -19,7 +19,8 @@ PICKED = 512
 SLOTS = 1024
 STRIP = 128
 HALF = SLOTS // 2
-CHUNKS = ((0, 128), (128, 128), (512, 256), (256, 256), (768, 256))
+CHUNKS = ((0, 128), (128, 128), (256, 256), (512, 256), (768, 256))
+QUARTER = SLOTS // 4
 BANK = 512
 
 FLOPS = 2 * 512 * 512 * 512 + 2 * 512 * 512 * 1024
@@ -47,17 +48,17 @@ def tile_picked_scorepage_none_po_kernel(
         kidx_sb = keep.tile([P, PICKED // 16], U16, name="kidx_sb")
         slot_sb = keep.tile([P, PICKED // 16], U16, name="slot_sb")
         offs_sb = keep.tile([P, PICKED // 16], U16, name="offs_sb")
-        d_tab = sbuf("d_tab", [P, TABLE], U32)
-        x_tab = sbuf("x_tab", [P, TABLE], U32)
+        d_tab = sbuf("d_tab", [P, TABLE], U32, "E")
+        x_tab = sbuf("x_tab", [P, TABLE], U32, "X")
         d_stab = sbuf("d_stab", [P, TABLE], U8, "A")
         x_stab = sbuf("x_stab", [P, TABLE], U8, "C")
         gn_sb = sbuf("gn_sb", [P, PACK], F32, "G")
         gn_kept = sbuf("gn_kept", [P, 1], F32)
-        page = [sbuf(f"page{t}", [P, SLOTS], F32) for t in range(3)]
+        page = [sbuf(f"page{t}", [P, SLOTS], F32) for t in range(2)]
         old_rows = old.rearrange("(p t) w -> t p w", t=PACK)
 
-        nc.vector.memset(d_stab[:].bitcast(I32), 0)
-        nc.gpsimd.memset(x_stab[:].bitcast(I32), 0)
+        nc.gpsimd.memset(d_stab[:].bitcast(I32), 0)
+        nc.vector.memset(x_stab[:].bitcast(I32), 0)
 
         nc.sync.dma_start(slot_sb[:], slot)
         nc.sync.dma_start(page[0][:], old_rows[0])
@@ -72,7 +73,6 @@ def tile_picked_scorepage_none_po_kernel(
             nc.sync.dma_start(x_stab[a:P:32, :].bitcast(I32), x_rows[a])
         nc.sync.dma_start(x_tab[:].bitcast(I32), words_of(x_words))
         nc.sync.dma_start(page[1][:], old_rows[1])
-        nc.sync.dma_start(page[2][:], old_rows[2])
         nc.gpsimd.dma_start(gn_sb[:], gn.rearrange("(p t) o -> p (t o)", t=PACK))
         nc.scalar.copy(gn_kept[:], gn_sb[:, PACK - 1 : PACK])
 
@@ -89,15 +89,17 @@ def tile_picked_scorepage_none_po_kernel(
         deal(nc, d_sc[:], d_sgot[:])
         for a in range(2):
             nc.scalar.dma_start(d_sc[2 + a : P : 32, :].bitcast(I32), d_sc[16 + a : P : 32, :].bitcast(I32))
-        page.append(sbuf("page3", [P, SLOTS], F32, "B"))
-        nc.sync.dma_start(page[3][:], old_rows[3])
+        page.append(sbuf("page2", [P, SLOTS], F32, "B"))
+        nc.sync.dma_start(page[2][:], old_rows[2])
 
         d_got = sbuf("d_got", [P, PICKED], U32, "D")
         d_codes = sbuf("d_codes", [P, PICKED], U32)
         nc.vector.tensor_copy(d_got[:], d_tab[:].indirect(kidx_sb[:]))
         x_sc = sbuf("x_sc", [P, PICKED], U8)
         nc.vector.tensor_copy(x_sc[:], x_stab[:].indirect(offs_sb[:]))
-        w_raw = sbuf("w_raw", [P, PICKED], U32, "C")
+        page.append(sbuf("page3", [P, SLOTS], F32, "C"))
+        nc.sync.dma_start(page[3][:], old_rows[3])
+        w_raw = sbuf("w_raw", [P, PICKED], U32, "E")
         nc.sync.dma_start(w_raw[:].bitcast(I32), words_of(w1_words))
         deal(nc, d_codes[:].bitcast(I32), d_got[:].bitcast(I32))
         w_sraw = sbuf("w_sraw", [P, PICKED], U8, "D")
@@ -120,9 +122,9 @@ def tile_picked_scorepage_none_po_kernel(
 
         z_bf = [sbuf(f"z_bf{h}", [P, HALF * PACK], BF16) for h in range(2)]
 
-        def z_plane(t, start, width):
-            at = start % HALF
-            return z_bf[start // HALF][:].rearrange("p (w t) -> p w t", t=PACK)[:, at : at + width, t]
+        def z_columns(start, width):
+            at = (start // HALF * QUARTER + start % QUARTER) * PACK
+            return z_bf[start // QUARTER % 2][:, at : at + width * PACK]
 
         new = {}
 
@@ -133,23 +135,21 @@ def tile_picked_scorepage_none_po_kernel(
         def put(t):
             nc.vector.tensor_copy(page[t][:].indirect(slot_sb[:]), new[t][:])
 
-        def weigh_on_scalar(t, start, width, gains):
-            nc.scalar.activation(z_plane(t, start, width), page[t][:, start : start + width], COPY, scale=gains)
-
         def weigh_early(t):
-            weigh_on_scalar(t, 0, HALF, gn_sb[:, t : t + 1])
-            weigh_on_scalar(t, HALF, HALF, gn_sb[:, t : t + 1])
+            quarters = page[t][:].rearrange("p (b h w) -> p h b w", b=2, h=2)
+            for h in range(2):
+                plane = z_bf[h][:].rearrange("p (b w t) -> p b w t", b=2, t=PACK)[:, :, :, t]
+                nc.scalar.activation(plane, quarters[:, h], COPY, scale=gn_sb[:, t : t + 1])
 
         def weigh_last(start, width):
             t = PACK - 1
-            if start >= HALF:
-                weigh_on_scalar(t, start, width, gn_last[:])
+            plane = z_columns(start, width).rearrange("p (w t) -> p w t", t=PACK)[:, :, t]
+            if start // QUARTER % 2:
+                nc.scalar.activation(plane, page[t][:, start : start + width], COPY, scale=gn_last[:])
             else:
-                nc.vector.tensor_scalar(
-                    z_plane(t, start, width), page[t][:, start : start + width], gn_last[:], None, ALU.mult
-                )
+                nc.vector.tensor_scalar(plane, page[t][:, start : start + width], gn_last[:], None, ALU.mult)
 
-        fetch(1)
+        fetch(1, "X")
         larger(0, "N0")
         larger(1, "N1")
         put(0)
@@ -178,10 +178,7 @@ def tile_picked_scorepage_none_po_kernel(
         def product(start, width):
             z_codes = sbuf(f"z_codes{start}", [P, width], U32)
             z_sc = sbuf(f"z_sc{start}", [P, width], U8)
-            at = start % HALF * PACK
-            nc.vector.quantize_mx(
-                out=z_codes[:].bitcast(FP8X4), scales=z_sc[:], in_=z_bf[start // HALF][:, at : at + width * PACK]
-            )
+            nc.vector.quantize_mx(out=z_codes[:].bitcast(FP8X4), scales=z_sc[:], in_=z_columns(start, width))
             n = STRIP if start == CHUNKS[-1][0] else width
             banks[start] = []
             for s in range(0, width, n):
@@ -209,30 +206,36 @@ def tile_picked_scorepage_none_po_kernel(
                 in_=source.rearrange("p t (g i) -> p g t i", i=4),
             )
 
+        y_late = sbuf("y_late", [P, PACK, HALF], F32)
+
         def leave(start, width):
-            y[start] = sbuf(f"y{start}", [P, PACK, width], F32)
+            if start < HALF:
+                y[start] = sbuf(f"y{start}", [P, PACK, width], F32)[:]
+            else:
+                y[start] = y_late[:, :, start - HALF : start - HALF + width]
             for bank, rows, strip in banks[start]:
-                if start + strip.stop == SLOTS:
-                    y_bf[SLOTS - STRIP] = sbuf("y_bf_last", [P, STRIP * PACK], BF16)
-                    nc.scalar.copy(
-                        out=y_bf[SLOTS - STRIP][:].rearrange("p (w t) -> p w t", t=PACK),
-                        in_=bank[:].rearrange("p t w -> p w t"),
-                    )
                 nc.scalar.copy(y[start][:, rows, strip], bank[:])
-            nc.sync.dma_start(out_rows[:, :, start : start + width], y[start][:])
+            if start < HALF:
+                nc.sync.dma_start(out_rows[:, :, start : start + width], y[start])
+            if start == last:
+                nc.sync.dma_start(out_rows[:, :, HALF:SLOTS], y_late[:])
+                y_bf[SLOTS - STRIP] = sbuf("y_bf_last", [P, STRIP * PACK], BF16)
+                nc.scalar.copy(
+                    out=y_bf[SLOTS - STRIP][:].rearrange("p (w t) -> p w t", t=PACK),
+                    in_=banks[start][-1][0][:].rearrange("p t w -> p w t"),
+                )
 
         def weave(start, width):
-            weave_from(start, y[start][:, :, 0:STRIP] if start == last else y[start][:])
+            weave_from(start, y[start][:, :, 0:STRIP] if start == last else y[start])
 
         def planes(start, width):
             parts = (start, start + STRIP) if start == last else (start,)
             for at in parts:
                 cols = slice(at, at + width // len(parts))
                 nc.vector.quantize_mx(out=y_codes[:, cols].bitcast(FP8X4), scales=y_sc[:, cols], in_=y_bf[at][:])
-            if start == CHUNKS[-2][0]:
-                nc.sync.dma_start(out_words[:, 0:last], y_codes[:, 0:last].bitcast(I32))
-            if start == last:
-                nc.sync.dma_start(out_words[:, last:SLOTS], y_codes[:, last:SLOTS].bitcast(I32))
+            if (start + width) % HALF == 0:
+                cols = slice(start + width - HALF, start + width)
+                nc.sync.dma_start(out_words[:, cols], y_codes[:, cols].bitcast(I32))
 
         stages = (weigh_last, product, leave, weave, planes)
         for step in range(len(CHUNKS) + len(stages) - 1):

from contextlib import ExitStack

import concourse.mybir as mybir

F32 = mybir.dt.float32
BF16 = mybir.dt.bfloat16
I32 = mybir.dt.int32
U32 = mybir.dt.uint32
U16 = mybir.dt.uint16
U8 = mybir.dt.uint8
FP8X4 = mybir.dt.float8_e4m3fn_x4
ALU = mybir.AluOpType
COPY = mybir.ActivationFunctionType.Copy

P = 128
PACK = 4
TABLE = 2048
PICKED = 512
SLOTS = 1024
STRIP = 128
HALF = SLOTS // 2
CHUNKS = ((0, 128), (128, 128), (256, 256), (512, 256), (768, 256))
QUARTER = SLOTS // 4
BANK = 512

FLOPS = 2 * 512 * 512 * 512 + 2 * 512 * 512 * 1024


def words_of(dram_words):
    return dram_words[0].rearrange("p n r -> p (n r)").bitcast(I32)


def deal(nc, out, in_):
    nc.vector.tensor_copy(out=out.rearrange("p (t m) -> p m t", t=PACK), in_=in_.rearrange("p (m t) -> p m t", t=PACK))


def tile_picked_scorepage_none_po_kernel(
    tc, x_words, x_scales, d_words, d_scales, old, gn, w1_words, w1_scales, offs, kidx, slot, out_0, out_1, out_2
):
    nc = tc.nc
    with ExitStack() as ctx:
        keep = ctx.enter_context(tc.tile_pool(name="keep", bufs=1))
        psum = ctx.enter_context(tc.psum_pool(name="psum", bufs=8))

        def sbuf(name, shape, dtype, tag=None):
            return keep.tile(shape, dtype, name=name, tag=tag or name, align_bytes=64)

        kidx_sb = keep.tile([P, PICKED // 16], U16, name="kidx_sb")
        slot_sb = keep.tile([P, PICKED // 16], U16, name="slot_sb")
        offs_sb = keep.tile([P, PICKED // 16], U16, name="offs_sb")
        d_tab = sbuf("d_tab", [P, TABLE], U32, "E")
        x_tab = sbuf("x_tab", [P, TABLE], U32, "X")
        d_stab = sbuf("d_stab", [P, TABLE], U8, "A")
        x_stab = sbuf("x_stab", [P, TABLE], U8, "C")
        gn_sb = sbuf("gn_sb", [P, PACK], F32, "G")
        gn_kept = sbuf("gn_kept", [P, 1], F32)
        page = [sbuf(f"page{t}", [P, SLOTS], F32) for t in range(2)]
        old_rows = old.rearrange("(p t) w -> t p w", t=PACK)

        nc.gpsimd.memset(d_stab[:].bitcast(I32), 0)
        nc.vector.memset(x_stab[:].bitcast(I32), 0)

        nc.sync.dma_start(slot_sb[:], slot)
        nc.sync.dma_start(page[0][:], old_rows[0])
        nc.sync.dma_start(kidx_sb[:], kidx)
        d_rows = d_scales[0].bitcast(I32).rearrange("(r a) n -> a r n", a=2)
        for a in range(2):
            nc.sync.dma_start(d_stab[a:P:16, :].bitcast(I32), d_rows[a])
        nc.sync.dma_start(d_tab[:].bitcast(I32), words_of(d_words))
        nc.sync.dma_start(offs_sb[:], offs)
        x_rows = x_scales[0].bitcast(I32).rearrange("(q a) n -> a q n", a=4)
        for a in range(4):
            nc.sync.dma_start(x_stab[a:P:32, :].bitcast(I32), x_rows[a])
        nc.sync.dma_start(x_tab[:].bitcast(I32), words_of(x_words))
        nc.sync.dma_start(page[1][:], old_rows[1])
        nc.gpsimd.dma_start(gn_sb[:], gn.rearrange("(p t) o -> p (t o)", t=PACK))
        nc.scalar.copy(gn_kept[:], gn_sb[:, PACK - 1 : PACK])

        half = {}

        def fetch(t, tag=None):
            half[t] = sbuf(f"half{t}", [P, PICKED], F32, tag)
            nc.vector.tensor_scalar(half[t][:], page[t][:].indirect(slot_sb[:]), 0.5, 0.0, ALU.mult, ALU.add)

        fetch(0)
        d_sgot = sbuf("d_sgot", [P, PICKED], U8, "B")
        d_sc = sbuf("d_sc", [P, PICKED], U8)
        nc.vector.tensor_copy(d_sgot[:], d_stab[:].indirect(kidx_sb[:]))
        deal(nc, d_sc[:], d_sgot[:])
        for a in range(2):
            nc.scalar.dma_start(d_sc[2 + a : P : 32, :].bitcast(I32), d_sc[16 + a : P : 32, :].bitcast(I32))
        page.append(sbuf("page2", [P, SLOTS], F32, "B"))
        nc.sync.dma_start(page[2][:], old_rows[2])

        d_got = sbuf("d_got", [P, PICKED], U32, "D")
        d_codes = sbuf("d_codes", [P, PICKED], U32)
        nc.vector.tensor_copy(d_got[:], d_tab[:].indirect(kidx_sb[:]))
        x_sc = sbuf("x_sc", [P, PICKED], U8)
        nc.vector.tensor_copy(x_sc[:], x_stab[:].indirect(offs_sb[:]))
        page.append(sbuf("page3", [P, SLOTS], F32, "C"))
        nc.sync.dma_start(page[3][:], old_rows[3])
        w_raw = sbuf("w_raw", [P, PICKED], U32, "E")
        nc.sync.dma_start(w_raw[:].bitcast(I32), words_of(w1_words))
        deal(nc, d_codes[:].bitcast(I32), d_got[:].bitcast(I32))
        w_sraw = sbuf("w_sraw", [P, PICKED], U8, "D")
        nc.gpsimd.memset(w_sraw[:].bitcast(I32), 0)
        w_rows = w1_scales[0].bitcast(I32).rearrange("(q a) n -> a q n", a=4)
        for a in range(4):
            nc.sync.dma_start(w_sraw[a:P:32, :].bitcast(I32), w_rows[a])
        x_codes = sbuf("x_codes", [P, PICKED], U32)
        nc.vector.tensor_copy(x_codes[:], x_tab[:].indirect(offs_sb[:]))

        scores = []
        for t in range(PACK):
            bank = psum.tile([P, PICKED], F32, name="bank")
            cols = slice(t * P, (t + 1) * P)
            nc.tensor.matmul_mx(
                out=bank[:], lhsT=d_codes[:, cols].bitcast(FP8X4), lhsT_scale=d_sc[:, cols],
                rhs=x_codes[:].bitcast(FP8X4), rhs_scale=x_sc[:], start=True, stop=True,
            )
            scores.append(bank)

        z_bf = [sbuf(f"z_bf{h}", [P, HALF * PACK], BF16) for h in range(2)]

        def z_columns(start, width):
            at = (start // HALF * QUARTER + start % QUARTER) * PACK
            return z_bf[start // QUARTER % 2][:, at : at + width * PACK]

        new = {}

        def larger(t, tag=None):
            new[t] = sbuf(f"new{t}", [P, PICKED], F32, tag)
            nc.vector.scalar_tensor_tensor(new[t][:], scores[t][:], 0.0625, half[t][:], ALU.mult, ALU.max)

        def put(t):
            nc.vector.tensor_copy(page[t][:].indirect(slot_sb[:]), new[t][:])

        def weigh_early(t):
            quarters = page[t][:].rearrange("p (b h w) -> p h b w", b=2, h=2)
            for h in range(2):
                plane = z_bf[h][:].rearrange("p (b w t) -> p b w t", b=2, t=PACK)[:, :, :, t]
                nc.scalar.activation(plane, quarters[:, h], COPY, scale=gn_sb[:, t : t + 1])

        def weigh_last(start, width):
            t = PACK - 1
            plane = z_columns(start, width).rearrange("p (w t) -> p w t", t=PACK)[:, :, t]
            if start // QUARTER % 2:
                nc.scalar.activation(plane, page[t][:, start : start + width], COPY, scale=gn_last[:])
            else:
                nc.vector.tensor_scalar(plane, page[t][:, start : start + width], gn_last[:], None, ALU.mult)

        fetch(1, "X")
        larger(0, "N0")
        larger(1, "N1")
        put(0)
        weigh_early(0)
        fetch(2, "N0")
        put(1)
        weigh_early(1)
        larger(2, "N2")
        fetch(3, "N1")
        put(2)
        weigh_early(2)
        gn_last = sbuf("gn_last", [P, 1], F32, "G")
        nc.scalar.copy(gn_last[:], gn_kept[:])
        larger(3, "N3")
        w_codes = sbuf("w_codes", [P, PICKED], U32, "N2")
        deal(nc, w_codes[:].bitcast(I32), w_raw[:].bitcast(I32))
        put(3)
        w_sc = sbuf("w_sc", [P, PICKED], U8, "N3")
        deal(nc, w_sc[:], w_sraw[:])

        y_sc = sbuf("y_sc", [P, SLOTS], U8)
        out_rows = out_0.rearrange("(p t) w -> p t w", t=PACK)
        out_words = words_of(out_1)
        banks = {}

        def product(start, width):
            z_codes = sbuf(f"z_codes{start}", [P, width], U32)
            z_sc = sbuf(f"z_sc{start}", [P, width], U8)
            nc.vector.quantize_mx(out=z_codes[:].bitcast(FP8X4), scales=z_sc[:], in_=z_columns(start, width))
            n = STRIP if start == CHUNKS[-1][0] else width
            banks[start] = []
            for s in range(0, width, n):
                strip = slice(s, s + n)
                for t in range(PACK):
                    if t % (BANK // n) == 0:
                        bank = psum.tile([P, BANK // n, n], F32, name="bank")
                        banks[start].append((bank, slice(t, t + BANK // n), strip))
                    cols = slice(t * P, (t + 1) * P)
                    nc.tensor.matmul_mx(
                        out=bank[:, t % (BANK // n), :], lhsT=w_codes[:, cols].bitcast(FP8X4), lhsT_scale=w_sc[:, cols],
                        rhs=z_codes[:, strip].bitcast(FP8X4), rhs_scale=z_sc[:, strip], start=True, stop=True,
                    )

        y = {}
        y_bf = {}
        y_codes = sbuf("y_codes", [P, SLOTS], U32)
        last = CHUNKS[-1][0]

        def weave_from(start, source):
            width = source.shape[-1]
            y_bf[start] = sbuf(f"y_bf{start}", [P, width * PACK], BF16)
            nc.vector.tensor_copy(
                out=y_bf[start][:].rearrange("p (g i t) -> p g t i", i=4, t=PACK),
                in_=source.rearrange("p t (g i) -> p g t i", i=4),
            )

        y_late = sbuf("y_late", [P, PACK, HALF], F32)

        def leave(start, width):
            if start < HALF:
                y[start] = sbuf(f"y{start}", [P, PACK, width], F32)[:]
            else:
                y[start] = y_late[:, :, start - HALF : start - HALF + width]
            for bank, rows, strip in banks[start]:
                nc.scalar.copy(y[start][:, rows, strip], bank[:])
            if start < HALF:
                nc.sync.dma_start(out_rows[:, :, start : start + width], y[start])
            if start == last:
                nc.sync.dma_start(out_rows[:, :, HALF:SLOTS], y_late[:])
                y_bf[SLOTS - STRIP] = sbuf("y_bf_last", [P, STRIP * PACK], BF16)
                nc.scalar.copy(
                    out=y_bf[SLOTS - STRIP][:].rearrange("p (w t) -> p w t", t=PACK),
                    in_=banks[start][-1][0][:].rearrange("p t w -> p w t"),
                )

        def weave(start, width):
            weave_from(start, y[start][:, :, 0:STRIP] if start == last else y[start])

        def planes(start, width):
            parts = (start, start + STRIP) if start == last else (start,)
            for at in parts:
                cols = slice(at, at + width // len(parts))
                nc.vector.quantize_mx(out=y_codes[:, cols].bitcast(FP8X4), scales=y_sc[:, cols], in_=y_bf[at][:])
            if (start + width) % HALF == 0:
                cols = slice(start + width - HALF, start + width)
                nc.sync.dma_start(out_words[:, cols], y_codes[:, cols].bitcast(I32))

        stages = (weigh_last, product, leave, weave, planes)
        for step in range(len(CHUNKS) + len(stages) - 1):
            for lag, stage in enumerate(stages):
                if 0 <= step - lag < len(CHUNKS):
                    stage(*CHUNKS[step - lag])
        out_srows = out_2[0].bitcast(I32).rearrange("(q a) n -> a q n", a=4)
        for a in range(4):
            queue = nc.scalar if a % 2 else nc.sync
            queue.dma_start(out_srows[a], y_sc[a:P:32, :].bitcast(I32))
